import numpy as np
import ml_dtypes


def mxq(x, axis, fmt="e4m3"):
    dtype, down = {"e4m3": (ml_dtypes.float8_e4m3fn, 7), "e5m2": (ml_dtypes.float8_e5m2, 14)}[fmt]
    v = np.moveaxis(np.asarray(x, np.float32).astype(ml_dtypes.bfloat16).astype(np.float64), axis, -1)
    blocks = v.reshape(v.shape[:-1] + (-1, 32))
    amax = np.abs(blocks).max(-1, keepdims=True)
    byte = np.maximum(np.where(amax > 0, np.frexp(amax)[1] - 1 + 127, 0) - down, 1)
    scale = np.exp2(byte - 127.0)
    codes = (blocks / scale).astype(np.float32).astype(dtype).astype(np.float64)
    return np.moveaxis((codes * scale).reshape(v.shape), -1, axis)


WIDE = False


def mx_kscale(k):
    if not WIDE:
        return np.ones(k)
    levels = np.array([10, -10, 5, -5, 0])
    if k % 512:
        return np.exp2(np.random.permutation(np.resize(levels, k // 32))).repeat(32)
    a = np.empty((k // 512, 16))
    for p in range(k // 512):
        a[p, :8] = np.random.permutation(np.resize(levels, 8))
        for g in range(8):
            far = levels[np.abs(levels - a[p, g]) >= 10]
            a[p, g + 8] = far[np.random.randint(len(far))]
    return np.exp2(a.ravel()).repeat(32)


def f64(x):
    return np.asarray(x).astype(np.float64)


def striped(idx):
    return np.tile(idx.reshape(-1, 16).T, (8, 1)).astype(np.uint16)


def unstriped(offs):
    return offs[:16].T.reshape(-1).astype(np.int64)


def striped8(idx):
    return np.concatenate([x.reshape(-1, 16).T for x in idx]).astype(np.uint16)


def runs(offs, k):
    lists = np.stack([offs[16 * r : 16 * r + 16].T.reshape(-1) for r in range(8)]).astype(np.int64)
    return lists[np.arange(k) % 512 // 64]


def pack_weight(w):
    k, n = w.shape
    w = f64(np.asarray(w, np.float32).astype(ml_dtypes.bfloat16)).reshape(k // 32, 32, n)
    amax = np.abs(w).max(1)
    byte = np.clip(np.where(amax > 0, np.frexp(amax)[1] - 1 + 127 - 7, 1), 1, 254)
    scaled = (w * np.exp2(127.0 - byte)[:, None, :]).reshape(k, n).astype(np.float32)
    words = np.ascontiguousarray(scaled.reshape(k // 512, 128, 4, n).transpose(0, 1, 3, 2)).astype(ml_dtypes.float8_e4m3fn).view(np.uint8)
    return words, np.ascontiguousarray(byte.astype(np.uint8).reshape(k // 512, 16, n))


def unpack_weight(words, scales):
    g, p, n, _ = words.shape
    vals = np.ascontiguousarray(words).view(ml_dtypes.float8_e4m3fn).astype(np.float64) * np.repeat(np.exp2(scales.astype(np.float64) - 127.0), 8, axis=1)[..., None]
    return vals.transpose(0, 1, 3, 2).reshape(g * 512, n)


K, T, S, V, N, H = 512, 2048, 512, 256, 512, 512


def setup_inputs():
    n = np.random.standard_normal
    s = mx_kscale(K)[:, None]
    u = mx_kscale(H)
    packed_xT = pack_weight(n((K, T)) * s)
    return {
        "x_words": packed_xT[0],
        "x_scales": packed_xT[1],
        "w1": (n((K, H)) / np.sqrt(K) / s).astype(np.float32),
        "w2": (n((K, H)) / np.sqrt(K) / s).astype(np.float32),
        "gn": (np.random.uniform(0.5, 1.5, (H, 1)) * u[:, None]).astype(np.float32),
        "w3": (n((H, N)) / np.sqrt(H) / u[:, None]).astype(np.float32),
        "res": (2 * n((N, V))).astype(np.float32),
        "offs": striped(np.random.permutation(T)[:S]),
        "two": striped(np.random.permutation(T)[:S]),
        "rule": striped8(np.random.randint(0, S, (8, V))),
        "l1": striped8(np.stack([np.random.permutation(S)[:V] for _ in range(8)])),
        "r1": striped8(np.stack([np.random.permutation(S)[:V] for _ in range(8)])),
        "l2": striped8(np.stack([np.random.permutation(S)[:V] for _ in range(8)])),
        "r2": striped8(np.stack([np.random.permutation(S)[:V] for _ in range(8)])),
    }


def reference(x_words, x_scales, w1, w2, gn, w3, res, offs, two, rule, l1, r1, l2, r2):
    xq = unpack_weight(x_words, x_scales)[:, unstriped(offs)]
    y = mxq(f64(w1), 0, "e4m3").T @ xq
    x_two = unpack_weight(x_words, x_scales)[:, unstriped(two)]
    c = mxq(f64(w2), 0, "e4m3").T @ x_two
    z = f64(gn) * (np.maximum(y[np.arange(H)[:, None], runs(l1, H)] + y[np.arange(H)[:, None], runs(r1, H)], y[np.arange(H)[:, None], runs(l2, H)] + y[np.arange(H)[:, None], runs(r2, H)]) + c[np.arange(H)[:, None], runs(rule, H)])
    return f64(res) + (mxq(f64(w3), 0, "e4m3").T @ mxq(z, 0, "e4m3"))

@@ -1,0 +1,168 @@
+from contextlib import ExitStack
+
+import concourse.mybir as mybir
+
+K, T, S, V, N, H = 512, 2048, 512, 256, 512, 512
+FLOPS = 2 * K * H * S * 2 + 2 * H * N * V
+
+F32 = mybir.dt.float32
+BF16 = mybir.dt.bfloat16
+I32 = mybir.dt.int32
+U32 = mybir.dt.uint32
+U16 = mybir.dt.uint16
+U8 = mybir.dt.uint8
+FP8X4 = mybir.dt.float8_e4m3fn_x4
+ADD = mybir.AluOpType.add
+MAX = mybir.AluOpType.max
+COPY = mybir.ActivationFunctionType.Copy
+
+P = 128
+PACK = 4
+HALF = V // 2
+
+
+def tile_picked_insidecky_none_p_kernel(tc, x_words, x_scales, w1, w2, gn, w3, res, offs, two, rule, l1, r1, l2, r2, out):
+    nc = tc.nc
+    with ExitStack() as ctx:
+        held = ctx.enter_context(tc.tile_pool(name="held", bufs=1))
+        psum = ctx.enter_context(tc.psum_pool(name="psum", bufs=1))
+
+        def load_list(name, src):
+            tile = held.tile(list(src.shape), U16, name=name)
+            nc.sync.dma_start(tile[:], src)
+            return tile
+
+        def load_weight(name, w):
+            raw = held.tile([P, PACK, 512], F32, name=name)
+            nc.sync.dma_start(raw[:], w.rearrange("(p j) c -> p j c", j=PACK))
+            return raw
+
+        def dealt_views(grouped, raw, m0, m1):
+            dst = grouped[:].rearrange("p (t m j) -> p m t j", t=PACK, j=PACK)[:, m0:m1]
+            src = raw[:].rearrange("p j (m t) -> p m t j", t=PACK)[:, m0:m1]
+            return dst, src
+
+        def quantize(name, grouped, width):
+            codes = held.tile([P, width], U32, name=name + "_codes", align_bytes=64)
+            scales = held.tile([P, width], U8, name=name + "_scales", align_bytes=64)
+            nc.vector.quantize_mx(out=codes[:].bitcast(FP8X4), scales=scales[:], in_=grouped)
+            return codes, scales
+
+        def product(acc, lhs, cols, rhs):
+            nc.tensor.matmul_mx(out=acc, lhsT=lhs[0][:, cols].bitcast(FP8X4), lhsT_scale=lhs[1][:, cols],
+                                rhs=rhs[0][:].bitcast(FP8X4), rhs_scale=rhs[1][:], start=True, stop=True)
+
+        offs_t = load_list("offs_t", offs)
+        two_t = load_list("two_t", two)
+        xs = held.tile([P, T], U8, name="xs")
+        nc.vector.memset(xs[:].bitcast(I32), 0)
+        w1_v = w1.rearrange("(p j) c -> p j c", j=PACK)
+        w1_lo = held.tile([P, PACK, 256], F32, name="w1_lo")
+        w1_hi = held.tile([P, PACK, 256], F32, name="w1_hi")
+        nc.sync.dma_start(w1_lo[:], w1_v[:, :, :256])
+        for q in range(4):
+            nc.sync.dma_start(xs[32 * q : 32 * q + 4, :].bitcast(I32), x_scales[0, 4 * q : 4 * q + 4, :].bitcast(I32))
+        nc.sync.dma_start(w1_hi[:], w1_v[:, :, 256:])
+        xw = held.tile([P, T], I32, name="xw")
+        nc.sync.dma_start(xw[:], x_words[0].rearrange("p n t -> p (n t)").bitcast(I32))
+        l1_t = load_list("l1_t", l1)
+        l2_t = load_list("l2_t", l2)
+        r1_t = load_list("r1_t", r1)
+        r2_t = load_list("r2_t", r2)
+        w2_raw = load_weight("w2_raw", w2)
+        w3_raw = load_weight("w3_raw", w3)
+        rule_t = load_list("rule_t", rule)
+        gain = held.tile([P, PACK], F32, name="gain")
+        nc.sync.dma_start(gain[:], gn.rearrange("(p t) o -> p (t o)", t=PACK))
+        res_t = held.tile([P, PACK, V], F32, name="res_t")
+        nc.sync.dma_start(res_t[:], res.rearrange("(b p) v -> p b v", p=P))
+
+        def pick_scales(name, lst):
+            tile = held.tile([P, S], U8, name=name, align_bytes=64)
+            nc.vector.tensor_copy(tile[:], xs[:].indirect(lst[:]))
+            return tile
+
+        def pick_words(name, lst):
+            tile = held.tile([P, S], U32, name=name, align_bytes=64)
+            nc.vector.tensor_copy(tile[:], xw[:].bitcast(U32).indirect(lst[:]))
+            return tile
+
+        xa_s = pick_scales("xa_s", offs_t)
+        xb_s = pick_scales("xb_s", two_t)
+        w1_b = held.tile([P, PACK * H], BF16, name="w1_b", align_bytes=64)
+        w1_d = w1_b[:].rearrange("p (t m j) -> p m t j", t=PACK, j=PACK)
+        nc.scalar.copy(w1_d[:, :64], w1_lo[:].rearrange("p j (m t) -> p m t j", t=PACK))
+        nc.scalar.copy(w1_d[:, 64:], w1_hi[:].rearrange("p j (m t) -> p m t j", t=PACK))
+        w1_q = quantize("w1", w1_b[:], H)
+        xa = (pick_words("xa_w", offs_t), xa_s)
+        xb = (pick_words("xb_w", two_t), xb_s)
+
+        def project(name, wq, x, t, bank):
+            acc = psum.tile([P, S], F32, name=name + "_acc", tag="bank%d" % bank)
+            product(acc[:], wq, slice(P * t, P * (t + 1)), x)
+            rows = held.tile([P, S], F32, name="%s%d" % (name, t))
+            nc.scalar.copy(rows[:], acc[:])
+            return rows
+
+        w2_b = held.tile([P, PACK * H], BF16, name="w2_b", tag="hold_w2", align_bytes=64)
+        y = [project("y", w1_q, xa, 0, 0), project("y", w1_q, xa, 1, 1)]
+        nc.scalar.copy(*dealt_views(w2_b, w2_raw, 0, 64))
+        y.append(project("y", w1_q, xa, 2, 2))
+        nc.scalar.copy(*dealt_views(w2_b, w2_raw, 64, 128))
+        y.append(project("y", w1_q, xa, 3, 3))
+        w3_b = held.tile([P, PACK * N], BF16, name="w3_b", align_bytes=64)
+        for h in range(2):
+            cols = slice(256 * h, 256 * (h + 1))
+            nc.scalar.copy(w3_b[:].rearrange("p (c j) -> p c j", j=PACK)[:, cols], w3_raw[:].rearrange("p j c -> p c j")[:, cols])
+
+        def splits(t, tag):
+            left = held.tile([P, 2 * V], F32, name="left%d" % t, tag=tag, align_bytes=64)
+            sums = held.tile([P, 2 * V], F32, name="sums%d" % t)
+            nc.vector.tensor_copy(left[:, :V], y[t][:].indirect(l1_t[:]))
+            nc.vector.tensor_copy(left[:, V:], y[t][:].indirect(l2_t[:]))
+            nc.vector.tensor_tensor(sums[:, :V], y[t][:].indirect(r1_t[:]), left[:, :V], ADD)
+            nc.vector.tensor_tensor(sums[:, V:], y[t][:].indirect(r2_t[:]), left[:, V:], ADD)
+            return sums
+
+        def larger(t, sums):
+            best = held.tile([P, V], F32, name="best%d" % t, tag="best%d" % t, align_bytes=64)
+            nc.vector.tensor_tensor(best[:], sums[:, :V], sums[:, V:], MAX)
+            return best
+
+        z_b = held.tile([P, PACK * V], BF16, name="z_b", align_bytes=64)
+        z_v = z_b[:].rearrange("p (v t) -> p v t", t=PACK)
+
+        def finish(t, c_t, best, v0, v1):
+            total = held.tile([P, v1 - v0], F32, name="total%d_%d" % (t, v0))
+            nc.vector.tensor_tensor(total[:], c_t[:].indirect(rule_t[:, v0 // 16 : v1 // 16]), best[:, v0:v1], ADD)
+            nc.scalar.activation(z_v[:, v0:v1, t], total[:], COPY, scale=gain[:, t : t + 1])
+
+        s0 = splits(0, "left0")
+        s1 = splits(1, "left1")
+        b0 = larger(0, s0)
+        w2_q = quantize("w2", w2_b[:], H)
+        b1 = larger(1, s1)
+        c = [project("c", w2_q, xb, t, 4 + t) for t in range(PACK)]
+        s2 = splits(2, "hold_w2")
+        w3_q = quantize("w3", w3_b[:], N)
+        b2 = larger(2, s2)
+        finish(0, c[0], b0, 0, V)
+        finish(1, c[1], b1, 0, V)
+        finish(2, c[2], b2, 0, V)
+        s3 = splits(3, "best0")
+        b3 = larger(3, s3)
+        for h in range(2):
+            finish(3, c[3], b3, HALF * h, HALF * (h + 1))
+        out_v = out.rearrange("(b p) v -> p b v", p=P)
+        accs = []
+        for h in range(2):
+            z_q = quantize("z%d" % h, z_b[:, PACK * HALF * h : PACK * HALF * (h + 1)], HALF)
+            acc = psum.tile([P, PACK, HALF], F32, name="out_acc", tag="bank%d" % h)
+            for b in range(PACK):
+                product(acc[:, b, :], w3_q, slice(P * b, P * (b + 1)), z_q)
+            accs.append(acc)
+        for h in range(2):
+            cols = slice(HALF * h, HALF * (h + 1))
+            result = held.tile([P, PACK, HALF], F32, name="result%d" % h)
+            nc.vector.tensor_tensor(result[:], accs[h][:], res_t[:, :, cols], ADD)
+            nc.sync.dma_start(out_v[:, :, cols], result[:])

@@ -1,6 +1,7 @@
 from contextlib import ExitStack
 
 import concourse.mybir as mybir
+from concourse.masks import make_identity
 
 K, T, S, V, N, H = 512, 2048, 512, 256, 512, 512
 FLOPS = 2 * K * H * S * 2 + 2 * H * N * V
@@ -13,6 +14,9 @@ U16 = mybir.dt.uint16
 U8 = mybir.dt.uint8
 FP8X4 = mybir.dt.float8_e4m3fn_x4
 ADD = mybir.AluOpType.add
+MULT = mybir.AluOpType.mult
+RELU = mybir.ActivationFunctionType.Relu
+SUB = mybir.AluOpType.subtract
 MAX = mybir.AluOpType.max
 COPY = mybir.ActivationFunctionType.Copy
 
@@ -33,7 +37,7 @@ def tile_picked_insidecky_none_p_kernel(tc, x_words, x_scales, w1, w2, gn, w3, r
             return tile
 
         def load_weight(name, w):
-            raw = held.tile([P, PACK, 512], F32, name=name)
+            raw = held.tile([P, PACK, 512], F32, name=name, tag=name)
             nc.sync.dma_start(raw[:], w.rearrange("(p j) c -> p j c", j=PACK))
             return raw
 
@@ -43,14 +47,21 @@ def tile_picked_insidecky_none_p_kernel(tc, x_words, x_scales, w1, w2, gn, w3, r
             return dst, src
 
         def quantize(name, grouped, width):
-            codes = held.tile([P, width], U32, name=name + "_codes", align_bytes=64)
+            codes = held.tile([P, width], U32, name=name + "_codes", tag=name + "_codes", align_bytes=64)
             scales = held.tile([P, width], U8, name=name + "_scales", align_bytes=64)
             nc.vector.quantize_mx(out=codes[:].bitcast(FP8X4), scales=scales[:], in_=grouped)
             return codes, scales
 
-        def product(acc, lhs, cols, rhs):
+        def product(acc, lhs, cols, words, scales):
             nc.tensor.matmul_mx(out=acc, lhsT=lhs[0][:, cols].bitcast(FP8X4), lhsT_scale=lhs[1][:, cols],
-                                rhs=rhs[0][:].bitcast(FP8X4), rhs_scale=rhs[1][:], start=True, stop=True)
+                                rhs=words.bitcast(FP8X4), rhs_scale=scales, start=True, stop=True)
+
+        ident = held.tile([P, P], F32, name="ident")
+        make_identity(nc, ident[:])
+
+        def turn_and_add(acc, parts):
+            for i, part in enumerate(parts):
+                nc.tensor.matmul(acc, part, ident[:], start=(i == 0), stop=(i == len(parts) - 1), is_transpose=True)
 
         offs_t = load_list("offs_t", offs)
         two_t = load_list("two_t", two)
@@ -61,7 +72,7 @@ def tile_picked_insidecky_none_p_kernel(tc, x_words, x_scales, w1, w2, gn, w3, r
         w1_hi = held.tile([P, PACK, 256], F32, name="w1_hi")
         nc.sync.dma_start(w1_lo[:], w1_v[:, :, :256])
         for q in range(4):
-            nc.sync.dma_start(xs[32 * q : 32 * q + 4, :].bitcast(I32), x_scales[0, 4 * q : 4 * q + 4, :].bitcast(I32))
+            nc.sync.dma_start(xs[q:P:32, :].bitcast(I32), x_scales[0, q:16:4, :].bitcast(I32))
         nc.sync.dma_start(w1_hi[:], w1_v[:, :, 256:])
         xw = held.tile([P, T], I32, name="xw")
         nc.sync.dma_start(xw[:], x_words[0].rearrange("p n t -> p (n t)").bitcast(I32))
@@ -70,7 +81,12 @@ def tile_picked_insidecky_none_p_kernel(tc, x_words, x_scales, w1, w2, gn, w3, r
         r1_t = load_list("r1_t", r1)
         r2_t = load_list("r2_t", r2)
         w2_raw = load_weight("w2_raw", w2)
-        w3_raw = load_weight("w3_raw", w3)
+        w3_v = w3.rearrange("(p j) c -> p j c", j=PACK)
+        w3_raw = []
+        for h in range(2):
+            raw = held.tile([P, PACK, 256], F32, name="w3_raw%d" % h, tag="w3_raw%d" % h)
+            nc.sync.dma_start(raw[:], w3_v[:, :, 256 * h : 256 * (h + 1)])
+            w3_raw.append(raw)
         rule_t = load_list("rule_t", rule)
         gain = held.tile([P, PACK], F32, name="gain")
         nc.sync.dma_start(gain[:], gn.rearrange("(p t) o -> p (t o)", t=PACK))
@@ -83,8 +99,8 @@ def tile_picked_insidecky_none_p_kernel(tc, x_words, x_scales, w1, w2, gn, w3, r
             return tile
 
         def pick_words(name, lst):
-            tile = held.tile([P, S], U32, name=name, align_bytes=64)
-            nc.vector.tensor_copy(tile[:], xw[:].bitcast(U32).indirect(lst[:]))
+            tile = held.tile([P, 16 * lst.shape[1]], U32, name=name, align_bytes=64)
+            nc.vector.tensor_copy(tile[:], xw[:].bitcast(U32).indirect(lst))
             return tile
 
         xa_s = pick_scales("xa_s", offs_t)
@@ -94,75 +110,114 @@ def tile_picked_insidecky_none_p_kernel(tc, x_words, x_scales, w1, w2, gn, w3, r
         nc.scalar.copy(w1_d[:, :64], w1_lo[:].rearrange("p j (m t) -> p m t j", t=PACK))
         nc.scalar.copy(w1_d[:, 64:], w1_hi[:].rearrange("p j (m t) -> p m t j", t=PACK))
         w1_q = quantize("w1", w1_b[:], H)
-        xa = (pick_words("xa_w", offs_t), xa_s)
-        xb = (pick_words("xb_w", two_t), xb_s)
+        xa_w = [pick_words("xa_w%d" % h, offs_t[:, 16 * h : 16 * (h + 1)]) for h in range(2)]
+        xb_w = pick_words("xb_w", two_t[:])
 
-        def project(name, wq, x, t, bank):
-            acc = psum.tile([P, S], F32, name=name + "_acc", tag="bank%d" % bank)
-            product(acc[:], wq, slice(P * t, P * (t + 1)), x)
-            rows = held.tile([P, S], F32, name="%s%d" % (name, t))
+        y_acc = [psum.tile([P, S], F32, name="y_acc%d" % t, tag="bank%d" % t) for t in range(PACK)]
+        y = [held.tile([P, S], F32, name="y%d" % t) for t in range(PACK)]
+        for tiles in ((0, 1), (2,), (3,)):
+            for h in range(2):
+                cols = slice(256 * h, 256 * (h + 1))
+                for t in tiles:
+                    product(y_acc[t][:, cols], w1_q, slice(P * t, P * (t + 1)), xa_w[h][:], xa_s[:, cols])
+                    if t < 2:
+                        nc.scalar.copy(y[t][:, cols], y_acc[t][:, cols])
+            if tiles[0] >= 2:
+                nc.scalar.copy(y[tiles[0]][:], y_acc[tiles[0]][:])
+
+        def project_c(t):
+            acc = psum.tile([P, S], F32, name="c_acc", tag="bank%d" % (4 + t))
+            product(acc[:], w2_q, slice(P * t, P * (t + 1)), xb_w[:], xb_s[:])
+            rows = held.tile([P, S], F32, name="c%d" % t, tag="w3_raw0" if t == 0 else "c%d" % t)
             nc.scalar.copy(rows[:], acc[:])
             return rows
 
-        w2_b = held.tile([P, PACK * H], BF16, name="w2_b", tag="hold_w2", align_bytes=64)
-        y = [project("y", w1_q, xa, 0, 0), project("y", w1_q, xa, 1, 1)]
-        nc.scalar.copy(*dealt_views(w2_b, w2_raw, 0, 64))
-        y.append(project("y", w1_q, xa, 2, 2))
-        nc.scalar.copy(*dealt_views(w2_b, w2_raw, 64, 128))
-        y.append(project("y", w1_q, xa, 3, 3))
-        w3_b = held.tile([P, PACK * N], BF16, name="w3_b", align_bytes=64)
-        for h in range(2):
-            cols = slice(256 * h, 256 * (h + 1))
-            nc.scalar.copy(w3_b[:].rearrange("p (c j) -> p c j", j=PACK)[:, cols], w3_raw[:].rearrange("p j c -> p c j")[:, cols])
-
-        def splits(t, tag):
-            left = held.tile([P, 2 * V], F32, name="left%d" % t, tag=tag, align_bytes=64)
-            sums = held.tile([P, 2 * V], F32, name="sums%d" % t)
-            nc.vector.tensor_copy(left[:, :V], y[t][:].indirect(l1_t[:]))
-            nc.vector.tensor_copy(left[:, V:], y[t][:].indirect(l2_t[:]))
-            nc.vector.tensor_tensor(sums[:, :V], y[t][:].indirect(r1_t[:]), left[:, :V], ADD)
-            nc.vector.tensor_tensor(sums[:, V:], y[t][:].indirect(r2_t[:]), left[:, V:], ADD)
-            return sums
-
-        def larger(t, sums):
-            best = held.tile([P, V], F32, name="best%d" % t, tag="best%d" % t, align_bytes=64)
-            nc.vector.tensor_tensor(best[:], sums[:, :V], sums[:, V:], MAX)
-            return best
-
         z_b = held.tile([P, PACK * V], BF16, name="z_b", align_bytes=64)
         z_v = z_b[:].rearrange("p (v t) -> p v t", t=PACK)
+        halves = [slice(HALF * h, HALF * (h + 1)) for h in range(2)]
 
-        def finish(t, c_t, best, v0, v1):
-            total = held.tile([P, v1 - v0], F32, name="total%d_%d" % (t, v0))
-            nc.vector.tensor_tensor(total[:], c_t[:].indirect(rule_t[:, v0 // 16 : v1 // 16]), best[:, v0:v1], ADD)
-            nc.scalar.activation(z_v[:, v0:v1, t], total[:], COPY, scale=gain[:, t : t + 1])
+        w2_b = held.tile([P, PACK * H], BF16, name="w2_b", align_bytes=64)
+        nc.scalar.copy(*dealt_views(w2_b, w2_raw, 0, 128))
 
-        s0 = splits(0, "left0")
-        s1 = splits(1, "left1")
-        b0 = larger(0, s0)
+        def cast_w3(h, tag):
+            grouped = held.tile([P, PACK * 256], BF16, name="w3_b%d" % h, tag=tag, align_bytes=64)
+            nc.scalar.copy(grouped[:].rearrange("p (c j) -> p c j", j=PACK), w3_raw[h][:].rearrange("p j c -> p c j"))
+            return grouped
+
+        w3_b0 = cast_w3(0, "w3_b0")
+
+        early = range(3)
+        left1 = [held.tile([P, V], F32, name="left1_%d" % t) for t in early]
+        first = [held.tile([P, V], F32, name="first_%d" % t) for t in early]
+        for t in early:
+            nc.vector.tensor_copy(left1[t][:], y[t][:].indirect(l1_t[:]))
+        for t in early:
+            nc.vector.tensor_tensor(first[t][:], y[t][:].indirect(r1_t[:]), left1[t][:], ADD)
         w2_q = quantize("w2", w2_b[:], H)
-        b1 = larger(1, s1)
-        c = [project("c", w2_q, xb, t, 4 + t) for t in range(PACK)]
-        s2 = splits(2, "hold_w2")
-        w3_q = quantize("w3", w3_b[:], N)
-        b2 = larger(2, s2)
-        finish(0, c[0], b0, 0, V)
-        finish(1, c[1], b1, 0, V)
-        finish(2, c[2], b2, 0, V)
-        s3 = splits(3, "best0")
-        b3 = larger(3, s3)
+        c = [project_c(t) for t in range(PACK)]
+        w3_b1 = cast_w3(1, "w2_codes")
+        parts = held.tile([P, 3, V], F32, name="parts", tag="w2_raw")
+        part = [parts[:, t, :] for t in early]
+        for t in early:
+            nc.vector.tensor_tensor(part[t], y[t][:].indirect(l2_t[:]), first[t][:], SUB)
+        gap = held.tile([P, 3, V], F32, name="gap")
+        over = [held.tile([P, V], F32, name="over_%d" % t) for t in early]
+        for t in early:
+            nc.vector.tensor_tensor(gap[:, t, :], y[t][:].indirect(r2_t[:]), part[t], ADD)
+        w3_q = [quantize("w3_0", w3_b0[:], 256)]
+        for t in early:
+            acc = psum.tile([P, V], F32, name="gap_acc", tag="bank%d" % (7 - t))
+            for cols in halves:
+                turn_and_add(acc[:, cols], [gap[:, t, cols]])
+            nc.scalar.activation(over[t][:], acc[:], RELU)
+
+        def base_of(t):
+            base = held.tile([P, V], F32, name="base_%d" % t)
+            nc.vector.tensor_tensor(base[:], c[t][:].indirect(rule_t[:]), first[t][:], ADD)
+            acc = psum.tile([P, V], F32, name="turned_acc", tag="bank%d" % t)
+            for cols in halves:
+                turn_and_add(acc[:, cols], [base[:, cols]])
+            turned = held.tile([P, V], F32, name="turned_%d" % t, tag="turned_%d" % t)
+            nc.scalar.copy(turned[:], acc[:])
+            return turned
+
+        def finish_turned(t, turned):
+            acc = psum.tile([P, V], F32, name="z_acc", tag="bank%d" % (4 + t))
+            for cols in halves:
+                turn_and_add(acc[:, cols], [over[t][:, cols], turned[:, cols]])
+            nc.scalar.activation(z_v[:, :, t], acc[:], COPY, scale=gain[:, t : t + 1])
+
+        turned0 = base_of(0)
+        turned1 = base_of(1)
+        finish_turned(0, turned0)
+        turned2 = base_of(2)
+        finish_turned(1, turned1)
+        finish_turned(2, turned2)
+        score = held.tile([P, V], F32, name="score")
+        nc.vector.tensor_copy(score[:], c[3][:].indirect(rule_t[:]))
+        w3_q.append(quantize("w3_1", w3_b1[:], 256))
+        left = held.tile([P, 2 * V], F32, name="left", tag="w3_raw1")
+        sums = held.tile([P, 2 * V], F32, name="sums")
+        nc.vector.tensor_tensor(left[:, :V], y[3][:].indirect(l1_t[:]), score[:], ADD)
+        nc.vector.tensor_tensor(left[:, V:], y[3][:].indirect(l2_t[:]), score[:], ADD)
+        nc.vector.tensor_tensor(sums[:, :V], y[3][:].indirect(r1_t[:]), left[:, :V], ADD)
         for h in range(2):
-            finish(3, c[3], b3, HALF * h, HALF * (h + 1))
+            cols = slice(V + HALF * h, V + HALF * (h + 1))
+            nc.vector.tensor_tensor(sums[:, cols], y[3][:].indirect(r2_t[:, 8 * h : 8 * (h + 1)]), left[:, cols], ADD)
+        best = held.tile([P, V], F32, name="best", tag="turned_2")
+        for h in range(2):
+            nc.vector.tensor_tensor(best[:, halves[h]], sums[:, HALF * h : HALF * (h + 1)], sums[:, V + HALF * h : V + HALF * (h + 1)], MAX)
+            nc.scalar.activation(z_v[:, halves[h], 3], best[:, halves[h]], COPY, scale=gain[:, 3:4])
         out_v = out.rearrange("(b p) v -> p b v", p=P)
-        accs = []
-        for h in range(2):
+        pieces = []
+        for h, groups in ((0, ((0, 4, 3),)), (1, ((0, 2, 7), (2, 4, 0)))):
             z_q = quantize("z%d" % h, z_b[:, PACK * HALF * h : PACK * HALF * (h + 1)], HALF)
-            acc = psum.tile([P, PACK, HALF], F32, name="out_acc", tag="bank%d" % h)
-            for b in range(PACK):
-                product(acc[:, b, :], w3_q, slice(P * b, P * (b + 1)), z_q)
-            accs.append(acc)
-        for h in range(2):
-            cols = slice(HALF * h, HALF * (h + 1))
-            result = held.tile([P, PACK, HALF], F32, name="result%d" % h)
-            nc.vector.tensor_tensor(result[:], accs[h][:], res_t[:, :, cols], ADD)
-            nc.sync.dma_start(out_v[:, :, cols], result[:])
+            for b0, b1, bank in groups:
+                acc = psum.tile([P, b1 - b0, HALF], F32, name="out_acc", tag="bank%d" % bank)
+                for b in range(b0, b1):
+                    product(acc[:, b - b0, :], w3_q[b // 2], slice(P * (b % 2), P * (b % 2 + 1)), z_q[0][:], z_q[1][:])
+                pieces.append((h, b0, b1, acc))
+        for h, b0, b1, acc in pieces:
+            result = held.tile([P, b1 - b0, HALF], F32, name="result%d_%d" % (h, b0))
+            nc.vector.tensor_tensor(result[:], acc[:], res_t[:, b0:b1, halves[h]], ADD)
+            nc.sync.dma_start(out_v[:, b0:b1, halves[h]], result[:])

@@ -29,6 +29,7 @@ def tile_picked_insidecky_none_p_kernel(tc, x_words, x_scales, w1, w2, gn, w3, r
     nc = tc.nc
     with ExitStack() as ctx:
         held = ctx.enter_context(tc.tile_pool(name="held", bufs=1))
+        head = ctx.enter_context(tc.tile_pool(name="head", bufs=1))
         psum = ctx.enter_context(tc.psum_pool(name="psum", bufs=1))
 
         def load_list(name, src):
@@ -37,7 +38,7 @@ def tile_picked_insidecky_none_p_kernel(tc, x_words, x_scales, w1, w2, gn, w3, r
             return tile
 
         def load_weight(name, w):
-            raw = held.tile([P, PACK, 512], F32, name=name, tag=name)
+            raw = held.tile([P, PACK, 512], F32, name=name, tag=name, align_bytes=64)
             nc.sync.dma_start(raw[:], w.rearrange("(p j) c -> p j c", j=PACK))
             return raw
 
@@ -67,15 +68,14 @@ def tile_picked_insidecky_none_p_kernel(tc, x_words, x_scales, w1, w2, gn, w3, r
         two_t = load_list("two_t", two)
         xs = held.tile([P, T], U8, name="xs")
         nc.vector.memset(xs[:].bitcast(I32), 0)
-        w1_v = w1.rearrange("(p j) c -> p j c", j=PACK)
-        w1_lo = held.tile([P, PACK, 256], F32, name="w1_lo")
-        w1_hi = held.tile([P, PACK, 256], F32, name="w1_hi")
-        nc.sync.dma_start(w1_lo[:], w1_v[:, :, :256])
+        xw = held.tile([P, T], I32, name="xw")
+        xw_v = x_words[0].rearrange("p n t -> p (n t)").bitcast(I32)
+        nc.sync.dma_start(xw[:, : T // 4], xw_v[:, : T // 4])
         for q in range(4):
             nc.sync.dma_start(xs[q:P:32, :].bitcast(I32), x_scales[0, q:16:4, :].bitcast(I32))
-        nc.sync.dma_start(w1_hi[:], w1_v[:, :, 256:])
-        xw = held.tile([P, T], I32, name="xw")
-        nc.sync.dma_start(xw[:], x_words[0].rearrange("p n t -> p (n t)").bitcast(I32))
+        w1_raw = head.tile([P, PACK, 512], F32, name="w1_raw", align_bytes=64, offset=0)
+        nc.sync.dma_start(w1_raw[:], w1.rearrange("(p j) c -> p j c", j=PACK))
+        nc.sync.dma_start(xw[:, T // 4 :], xw_v[:, T // 4 :])
         l1_t = load_list("l1_t", l1)
         l2_t = load_list("l2_t", l2)
         r1_t = load_list("r1_t", r1)
@@ -98,20 +98,17 @@ def tile_picked_insidecky_none_p_kernel(tc, x_words, x_scales, w1, w2, gn, w3, r
             nc.vector.tensor_copy(tile[:], xs[:].indirect(lst[:]))
             return tile
 
-        def pick_words(name, lst):
-            tile = held.tile([P, 16 * lst.shape[1]], U32, name=name, align_bytes=64)
-            nc.vector.tensor_copy(tile[:], xw[:].bitcast(U32).indirect(lst))
-            return tile
-
         xa_s = pick_scales("xa_s", offs_t)
         xb_s = pick_scales("xb_s", two_t)
         w1_b = held.tile([P, PACK * H], BF16, name="w1_b", align_bytes=64)
-        w1_d = w1_b[:].rearrange("p (t m j) -> p m t j", t=PACK, j=PACK)
-        nc.scalar.copy(w1_d[:, :64], w1_lo[:].rearrange("p j (m t) -> p m t j", t=PACK))
-        nc.scalar.copy(w1_d[:, 64:], w1_hi[:].rearrange("p j (m t) -> p m t j", t=PACK))
+        nc.scalar.copy(*dealt_views(w1_b, w1_raw, 0, 48))
+        nc.vector.tensor_copy(*dealt_views(w1_b, w1_raw, 48, 128))
         w1_q = quantize("w1", w1_b[:], H)
-        xa_w = [pick_words("xa_w%d" % h, offs_t[:, 16 * h : 16 * (h + 1)]) for h in range(2)]
-        xb_w = pick_words("xb_w", two_t[:])
+        xa_w = [head.tile([P, 256], U32, name="xa_w%d" % h, align_bytes=64, offset=1024 * h) for h in range(2)]
+        for h in range(2):
+            nc.vector.tensor_copy(xa_w[h][:], xw[:].bitcast(U32).indirect(offs_t[:, 16 * h : 16 * (h + 1)]))
+        xb_w = head.tile([P, S], U32, name="xb_w", align_bytes=64, offset=2048)
+        nc.vector.tensor_copy(xb_w[:], xw[:].bitcast(U32).indirect(two_t[:]))
 
         y_acc = [psum.tile([P, S], F32, name="y_acc%d" % t, tag="bank%d" % t) for t in range(PACK)]
         y = [held.tile([P, S], F32, name="y%d" % t) for t in range(PACK)]
@@ -141,7 +138,7 @@ def tile_picked_insidecky_none_p_kernel(tc, x_words, x_scales, w1, w2, gn, w3, r
 
         def cast_w3(h, tag):
             grouped = held.tile([P, PACK * 256], BF16, name="w3_b%d" % h, tag=tag, align_bytes=64)
-            nc.scalar.copy(grouped[:].rearrange("p (c j) -> p c j", j=PACK), w3_raw[h][:].rearrange("p j c -> p c j"))
+            nc.scalar.copy(grouped[:].rearrange("p (c i j) -> p c j i", i=4, j=PACK), w3_raw[h][:].rearrange("p j (c i) -> p c j i", i=4))
             return grouped
 
         w3_b0 = cast_w3(0, "w3_b0")
@@ -156,7 +153,7 @@ def tile_picked_insidecky_none_p_kernel(tc, x_words, x_scales, w1, w2, gn, w3, r
         w2_q = quantize("w2", w2_b[:], H)
         c = [project_c(t) for t in range(PACK)]
         w3_b1 = cast_w3(1, "w2_codes")
-        parts = held.tile([P, 3, V], F32, name="parts", tag="w2_raw")
+        parts = held.tile([P, 3, V], F32, name="parts", tag="w2_raw", align_bytes=64)
         part = [parts[:, t, :] for t in early]
         for t in early:
             nc.vector.tensor_tensor(part[t], y[t][:].indirect(l2_t[:]), first[t][:], SUB)

from contextlib import ExitStack

import concourse.mybir as mybir
from concourse.masks import make_identity

K, T, S, V, N, H = 512, 2048, 512, 256, 512, 512
FLOPS = 2 * K * H * S * 2 + 2 * H * N * V

F32 = mybir.dt.float32
BF16 = mybir.dt.bfloat16
I32 = mybir.dt.int32
U32 = mybir.dt.uint32
U16 = mybir.dt.uint16
U8 = mybir.dt.uint8
FP8X4 = mybir.dt.float8_e4m3fn_x4
ADD = mybir.AluOpType.add
MULT = mybir.AluOpType.mult
RELU = mybir.ActivationFunctionType.Relu
SUB = mybir.AluOpType.subtract
MAX = mybir.AluOpType.max
COPY = mybir.ActivationFunctionType.Copy

P = 128
PACK = 4
HALF = V // 2


def tile_picked_insidecky_none_p_kernel(tc, x_words, x_scales, w1, w2, gn, w3, res, offs, two, rule, l1, r1, l2, r2, out):
    nc = tc.nc
    with ExitStack() as ctx:
        held = ctx.enter_context(tc.tile_pool(name="held", bufs=1))
        head = ctx.enter_context(tc.tile_pool(name="head", bufs=1))
        psum = ctx.enter_context(tc.psum_pool(name="psum", bufs=1))

        def load_list(name, src):
            tile = held.tile(list(src.shape), U16, name=name)
            nc.sync.dma_start(tile[:], src)
            return tile

        def load_weight(name, w):
            raw = held.tile([P, PACK, 512], F32, name=name, tag=name, align_bytes=64)
            nc.sync.dma_start(raw[:], w.rearrange("(p j) c -> p j c", j=PACK))
            return raw

        def dealt_views(grouped, raw, m0, m1):
            dst = grouped[:].rearrange("p (t m j) -> p m t j", t=PACK, j=PACK)[:, m0:m1]
            src = raw[:].rearrange("p j (m t) -> p m t j", t=PACK)[:, m0:m1]
            return dst, src

        def quantize(name, grouped, width):
            codes = held.tile([P, width], U32, name=name + "_codes", tag=name + "_codes", align_bytes=64)
            scales = held.tile([P, width], U8, name=name + "_scales", align_bytes=64)
            nc.vector.quantize_mx(out=codes[:].bitcast(FP8X4), scales=scales[:], in_=grouped)
            return codes, scales

        def product(acc, lhs, cols, words, scales):
            nc.tensor.matmul_mx(out=acc, lhsT=lhs[0][:, cols].bitcast(FP8X4), lhsT_scale=lhs[1][:, cols],
                                rhs=words.bitcast(FP8X4), rhs_scale=scales, start=True, stop=True)

        ident = held.tile([P, P], F32, name="ident")
        make_identity(nc, ident[:])

        def turn_and_add(acc, parts):
            for i, part in enumerate(parts):
                nc.tensor.matmul(acc, part, ident[:], start=(i == 0), stop=(i == len(parts) - 1), is_transpose=True)

        offs_t = load_list("offs_t", offs)
        two_t = load_list("two_t", two)
        xs = held.tile([P, T], U8, name="xs")
        nc.vector.memset(xs[:].bitcast(I32), 0)
        xw = held.tile([P, T], I32, name="xw")
        xw_v = x_words[0].rearrange("p n t -> p (n t)").bitcast(I32)
        nc.sync.dma_start(xw[:, : T // 4], xw_v[:, : T // 4])
        for q in range(4):
            nc.sync.dma_start(xs[q:P:32, :].bitcast(I32), x_scales[0, q:16:4, :].bitcast(I32))
        w1_raw = head.tile([P, PACK, 512], F32, name="w1_raw", align_bytes=64, offset=0)
        nc.sync.dma_start(w1_raw[:], w1.rearrange("(p j) c -> p j c", j=PACK))
        nc.sync.dma_start(xw[:, T // 4 :], xw_v[:, T // 4 :])
        l1_t = load_list("l1_t", l1)
        l2_t = load_list("l2_t", l2)
        r1_t = load_list("r1_t", r1)
        r2_t = load_list("r2_t", r2)
        w2_raw = load_weight("w2_raw", w2)
        w3_v = w3.rearrange("(p j) c -> p j c", j=PACK)
        w3_raw = []
        for h in range(2):
            raw = held.tile([P, PACK, 256], F32, name="w3_raw%d" % h, tag="w3_raw%d" % h)
            nc.sync.dma_start(raw[:], w3_v[:, :, 256 * h : 256 * (h + 1)])
            w3_raw.append(raw)
        rule_t = load_list("rule_t", rule)
        gain = held.tile([P, PACK], F32, name="gain")
        nc.sync.dma_start(gain[:], gn.rearrange("(p t) o -> p (t o)", t=PACK))
        res_t = held.tile([P, PACK, V], F32, name="res_t")
        nc.sync.dma_start(res_t[:], res.rearrange("(b p) v -> p b v", p=P))

        def pick_scales(name, lst):
            tile = held.tile([P, S], U8, name=name, align_bytes=64)
            nc.vector.tensor_copy(tile[:], xs[:].indirect(lst[:]))
            return tile

        xa_s = pick_scales("xa_s", offs_t)
        xb_s = pick_scales("xb_s", two_t)
        w1_b = held.tile([P, PACK * H], BF16, name="w1_b", align_bytes=64)
        nc.scalar.copy(*dealt_views(w1_b, w1_raw, 0, 48))
        nc.vector.tensor_copy(*dealt_views(w1_b, w1_raw, 48, 128))
        w1_q = quantize("w1", w1_b[:], H)
        xa_w = [head.tile([P, 256], U32, name="xa_w%d" % h, align_bytes=64, offset=1024 * h) for h in range(2)]
        for h in range(2):
            nc.vector.tensor_copy(xa_w[h][:], xw[:].bitcast(U32).indirect(offs_t[:, 16 * h : 16 * (h + 1)]))
        xb_w = head.tile([P, S], U32, name="xb_w", align_bytes=64, offset=2048)
        nc.vector.tensor_copy(xb_w[:], xw[:].bitcast(U32).indirect(two_t[:]))

        y_acc = [psum.tile([P, S], F32, name="y_acc%d" % t, tag="bank%d" % t) for t in range(PACK)]
        y = [held.tile([P, S], F32, name="y%d" % t) for t in range(PACK)]
        for tiles in ((0, 1), (2,), (3,)):
            for h in range(2):
                cols = slice(256 * h, 256 * (h + 1))
                for t in tiles:
                    product(y_acc[t][:, cols], w1_q, slice(P * t, P * (t + 1)), xa_w[h][:], xa_s[:, cols])
                    if t < 2:
                        nc.scalar.copy(y[t][:, cols], y_acc[t][:, cols])
            if tiles[0] >= 2:
                nc.scalar.copy(y[tiles[0]][:], y_acc[tiles[0]][:])

        def project_c(t):
            acc = psum.tile([P, S], F32, name="c_acc", tag="bank%d" % (4 + t))
            product(acc[:], w2_q, slice(P * t, P * (t + 1)), xb_w[:], xb_s[:])
            rows = held.tile([P, S], F32, name="c%d" % t, tag="w3_raw0" if t == 0 else "c%d" % t)
            nc.scalar.copy(rows[:], acc[:])
            return rows

        z_b = held.tile([P, PACK * V], BF16, name="z_b", align_bytes=64)
        z_v = z_b[:].rearrange("p (v t) -> p v t", t=PACK)
        halves = [slice(HALF * h, HALF * (h + 1)) for h in range(2)]

        w2_b = held.tile([P, PACK * H], BF16, name="w2_b", align_bytes=64)
        nc.scalar.copy(*dealt_views(w2_b, w2_raw, 0, 128))

        def cast_w3(h, tag):
            grouped = held.tile([P, PACK * 256], BF16, name="w3_b%d" % h, tag=tag, align_bytes=64)
            nc.scalar.copy(grouped[:].rearrange("p (c i j) -> p c j i", i=4, j=PACK), w3_raw[h][:].rearrange("p j (c i) -> p c j i", i=4))
            return grouped

        w3_b0 = cast_w3(0, "w3_b0")

        early = range(3)
        left1 = [held.tile([P, V], F32, name="left1_%d" % t) for t in early]
        first = [held.tile([P, V], F32, name="first_%d" % t) for t in early]
        for t in early:
            nc.vector.tensor_copy(left1[t][:], y[t][:].indirect(l1_t[:]))
        for t in early:
            nc.vector.tensor_tensor(first[t][:], y[t][:].indirect(r1_t[:]), left1[t][:], ADD)
        w2_q = quantize("w2", w2_b[:], H)
        c = [project_c(t) for t in range(PACK)]
        w3_b1 = cast_w3(1, "w2_codes")
        parts = held.tile([P, 3, V], F32, name="parts", tag="w2_raw", align_bytes=64)
        part = [parts[:, t, :] for t in early]
        for t in early:
            nc.vector.tensor_tensor(part[t], y[t][:].indirect(l2_t[:]), first[t][:], SUB)
        gap = held.tile([P, 3, V], F32, name="gap")
        over = [held.tile([P, V], F32, name="over_%d" % t) for t in early]
        for t in early:
            nc.vector.tensor_tensor(gap[:, t, :], y[t][:].indirect(r2_t[:]), part[t], ADD)
        w3_q = [quantize("w3_0", w3_b0[:], 256)]
        for t in early:
            acc = psum.tile([P, V], F32, name="gap_acc", tag="bank%d" % (7 - t))
            for cols in halves:
                turn_and_add(acc[:, cols], [gap[:, t, cols]])
            nc.scalar.activation(over[t][:], acc[:], RELU)

        def base_of(t):
            base = held.tile([P, V], F32, name="base_%d" % t)
            nc.vector.tensor_tensor(base[:], c[t][:].indirect(rule_t[:]), first[t][:], ADD)
            acc = psum.tile([P, V], F32, name="turned_acc", tag="bank%d" % t)
            for cols in halves:
                turn_and_add(acc[:, cols], [base[:, cols]])
            turned = held.tile([P, V], F32, name="turned_%d" % t, tag="turned_%d" % t)
            nc.scalar.copy(turned[:], acc[:])
            return turned

        def finish_turned(t, turned):
            acc = psum.tile([P, V], F32, name="z_acc", tag="bank%d" % (4 + t))
            for cols in halves:
                turn_and_add(acc[:, cols], [over[t][:, cols], turned[:, cols]])
            nc.scalar.activation(z_v[:, :, t], acc[:], COPY, scale=gain[:, t : t + 1])

        turned0 = base_of(0)
        turned1 = base_of(1)
        finish_turned(0, turned0)
        turned2 = base_of(2)
        finish_turned(1, turned1)
        finish_turned(2, turned2)
        score = held.tile([P, V], F32, name="score")
        nc.vector.tensor_copy(score[:], c[3][:].indirect(rule_t[:]))
        w3_q.append(quantize("w3_1", w3_b1[:], 256))
        left = held.tile([P, 2 * V], F32, name="left", tag="w3_raw1")
        sums = held.tile([P, 2 * V], F32, name="sums")
        nc.vector.tensor_tensor(left[:, :V], y[3][:].indirect(l1_t[:]), score[:], ADD)
        nc.vector.tensor_tensor(left[:, V:], y[3][:].indirect(l2_t[:]), score[:], ADD)
        nc.vector.tensor_tensor(sums[:, :V], y[3][:].indirect(r1_t[:]), left[:, :V], ADD)
        for h in range(2):
            cols = slice(V + HALF * h, V + HALF * (h + 1))
            nc.vector.tensor_tensor(sums[:, cols], y[3][:].indirect(r2_t[:, 8 * h : 8 * (h + 1)]), left[:, cols], ADD)
        best = held.tile([P, V], F32, name="best", tag="turned_2")
        for h in range(2):
            nc.vector.tensor_tensor(best[:, halves[h]], sums[:, HALF * h : HALF * (h + 1)], sums[:, V + HALF * h : V + HALF * (h + 1)], MAX)
            nc.scalar.activation(z_v[:, halves[h], 3], best[:, halves[h]], COPY, scale=gain[:, 3:4])
        out_v = out.rearrange("(b p) v -> p b v", p=P)
        pieces = []
        for h, groups in ((0, ((0, 4, 3),)), (1, ((0, 2, 7), (2, 4, 0)))):
            z_q = quantize("z%d" % h, z_b[:, PACK * HALF * h : PACK * HALF * (h + 1)], HALF)
            for b0, b1, bank in groups:
                acc = psum.tile([P, b1 - b0, HALF], F32, name="out_acc", tag="bank%d" % bank)
                for b in range(b0, b1):
                    product(acc[:, b - b0, :], w3_q[b // 2], slice(P * (b % 2), P * (b % 2 + 1)), z_q[0][:], z_q[1][:])
                pieces.append((h, b0, b1, acc))
        for h, b0, b1, acc in pieces:
            result = held.tile([P, b1 - b0, HALF], F32, name="result%d_%d" % (h, b0))
            nc.vector.tensor_tensor(result[:], acc[:], res_t[:, b0:b1, halves[h]], ADD)
            nc.sync.dma_start(out_v[:, b0:b1, halves[h]], result[:])
